import numpy as np
import ml_dtypes


def mxq(x, axis, fmt="e4m3"):
    dtype, down = {"e4m3": (ml_dtypes.float8_e4m3fn, 7), "e5m2": (ml_dtypes.float8_e5m2, 14)}[fmt]
    v = np.moveaxis(np.asarray(x, np.float32).astype(ml_dtypes.bfloat16).astype(np.float64), axis, -1)
    blocks = v.reshape(v.shape[:-1] + (-1, 32))
    amax = np.abs(blocks).max(-1, keepdims=True)
    byte = np.maximum(np.where(amax > 0, np.frexp(amax)[1] - 1 + 127, 0) - down, 1)
    scale = np.exp2(byte - 127.0)
    codes = (blocks / scale).astype(np.float32).astype(dtype).astype(np.float64)
    return np.moveaxis((codes * scale).reshape(v.shape), -1, axis)


WIDE = False


def mx_kscale(k):
    if not WIDE:
        return np.ones(k)
    levels = np.array([10, -10, 5, -5, 0])
    if k % 512:
        return np.exp2(np.random.permutation(np.resize(levels, k // 32))).repeat(32)
    a = np.empty((k // 512, 16))
    for p in range(k // 512):
        a[p, :8] = np.random.permutation(np.resize(levels, 8))
        for g in range(8):
            far = levels[np.abs(levels - a[p, g]) >= 10]
            a[p, g + 8] = far[np.random.randint(len(far))]
    return np.exp2(a.ravel()).repeat(32)


def f64(x):
    return np.asarray(x).astype(np.float64)


def striped8(idx):
    return np.asarray(idx).reshape(8, -1, 16).transpose(0, 2, 1).reshape(128, -1).astype(np.uint16)


def unstriped8(offs):
    return offs.reshape(8, 16, -1).transpose(0, 2, 1).reshape(8, -1).astype(np.int64)


def pick8(x, idx, run):
    r = np.arange(len(x))
    return x[r[:, None], idx[r % (8 * run) // run]]


E2M1 = np.array([0.0, 0.5, 1.0, 1.5, 2.0, 3.0, 4.0, 6.0, -0.0, -0.5, -1.0, -1.5, -2.0, -3.0, -4.0, -6.0])


def pack_weight(w, fmt):
    k, n = w.shape
    w = f64(np.asarray(w, np.float32).astype(ml_dtypes.bfloat16)).reshape(k // 32, 32, n)
    amax = np.abs(w).max(1)
    if fmt == "e4m3":
        byte = np.frexp(amax)[1] - 1 + 127 - 7
    else:
        mant, ex = np.frexp(amax / 6.0)
        byte = np.where(mant > 0.5, ex, ex - 1) + 127
    byte = np.clip(np.where(amax > 0, byte, 1), 1, 254)
    scaled = (w * np.exp2(127.0 - byte)[:, None, :]).reshape(k, n).astype(np.float32)
    by_word = np.ascontiguousarray(scaled.reshape(k // 512, 128, 4, n).transpose(0, 1, 3, 2))
    if fmt == "e4m3":
        words = by_word.astype(ml_dtypes.float8_e4m3fn).view(np.uint8)
    else:
        c = by_word.astype(ml_dtypes.float4_e2m1fn).view(np.uint8) & 0xF
        words = (c[..., 0::2] | (c[..., 1::2] << 4)).reshape(k // 512, 128, 2 * n)
    return np.ascontiguousarray(words), np.ascontiguousarray(byte.astype(np.uint8).reshape(k // 512, 16, n))


def unpack_weight(words, scales, fmt):
    g, _, n = scales.shape
    words = np.ascontiguousarray(words).reshape(g, 128, n, -1)
    if fmt == "e4m3":
        vals = words.view(ml_dtypes.float8_e4m3fn).astype(np.float64)
    else:
        nib = np.empty((g, 128, n, 4), np.uint8)
        nib[..., 0::2] = words & 0xF
        nib[..., 1::2] = words >> 4
        vals = E2M1[nib]
    vals = vals * np.repeat(np.exp2(scales.astype(np.float64) - 127.0), 8, axis=1)[..., None]
    return vals.transpose(0, 1, 3, 2).reshape(g * 512, n)


D, K, T, U, X, S, I, Q = 512, 512, 1024, 1024, 1024, 1024, 512, 128


def setup_inputs():
    n = np.random.standard_normal
    idx = np.stack([np.random.permutation(T)[:I] for _ in range(8)])
    idx2 = np.stack([np.random.permutation(U)[:I] for _ in range(8)])
    idx3 = np.stack([np.random.permutation(X)[:I] for _ in range(8)])
    idx4 = np.stack([np.random.permutation(X)[:I] for _ in range(8)])
    idx5 = np.stack([np.random.permutation(S)[:I] for _ in range(8)])
    idx6 = np.stack([np.random.permutation(S)[:I] for _ in range(8)])
    fd = mx_kscale(D)
    fk = mx_kscale(K)
    wqp = pack_weight(n((D, K)) * 1.0 / np.sqrt(D) * fd[:, None] * fk, "e4m3")
    keysp = pack_weight(n((K, T)) * 1.0 / np.sqrt(K) / fk[:, None], "e4m3")
    notesp = pack_weight(n((K, U)) * 1.0 / np.sqrt(K) / fk[:, None], "e2m1")
    usersp = pack_weight(n((D, X)) * 1.0 / np.sqrt(D) * fd[:, None], "e4m3")
    shelvesp = pack_weight(n((D, S)) * 1.0 / np.sqrt(D) * fd[:, None], "e2m1")
    return {
        "states": (n((D, Q)) * 0.95 / fd[:, None]).astype(np.float32),
        "wq_words": wqp[0],
        "wq_scales": wqp[1],
        "keys_words": keysp[0],
        "keys_scales": keysp[1],
        "notes_words": notesp[0],
        "notes_scales": notesp[1],
        "users_words": usersp[0],
        "users_scales": usersp[1],
        "shelves_words": shelvesp[0],
        "shelves_scales": shelvesp[1],
        "offs": striped8(idx),
        "offs2": striped8(idx2),
        "offs3": striped8(idx3),
        "offs4": striped8(idx4),
        "offs5": striped8(idx5),
        "offs6": striped8(idx6),
    }


def reference(states, wq_words, wq_scales, keys_words, keys_scales, notes_words, notes_scales, users_words, users_scales, shelves_words, shelves_scales, offs, offs2, offs3, offs4, offs5, offs6):
    idx = unstriped8(offs)
    idx2 = unstriped8(offs2)
    idx3 = unstriped8(offs3)
    idx4 = unstriped8(offs4)
    idx5 = unstriped8(offs5)
    idx6 = unstriped8(offs6)
    wqu = unpack_weight(wq_words, wq_scales, "e4m3")
    keysu = unpack_weight(keys_words, keys_scales, "e4m3")
    notesu = unpack_weight(notes_words, notes_scales, "e2m1")
    usersu = unpack_weight(users_words, users_scales, "e4m3")
    shelvesu = unpack_weight(shelves_words, shelves_scales, "e2m1")
    statesq = mxq(f64(states), 0, "e4m3")
    qv = wqu.T @ statesq
    qvq = mxq(qv, 0, "e4m3")
    a = qvq.T @ keysu
    b = qvq.T @ notesu
    c0 = statesq.T @ usersu
    d0 = statesq.T @ shelvesu
    w = pick8(a, idx, 16) + pick8(b, idx2, 16)
    f1 = np.zeros((Q, X))
    f1[np.arange(Q)[:, None], idx3[np.arange(Q) % 128 // 16]] = w
    cc = c0 + f1
    v = pick8(cc, idx4, 16) - pick8(d0, idx5, 16)
    f2 = np.zeros((Q, S))
    f2[np.arange(Q)[:, None], idx6[np.arange(Q) % 128 // 16]] = v
    dd = d0 + f2
    y = pick8(dd, idx5, 16)
    return y

@@ -1,0 +1,185 @@
+from contextlib import ExitStack
+
+import concourse.mybir as mybir
+
+F32 = mybir.dt.float32
+BF16 = mybir.dt.bfloat16
+I32 = mybir.dt.int32
+U32 = mybir.dt.uint32
+U16 = mybir.dt.uint16
+U8 = mybir.dt.uint8
+FP8X4 = mybir.dt.float8_e4m3fn_x4
+FP4X4 = mybir.dt.float4_e2m1fn_x4
+ADD = mybir.AluOpType.add
+COPY = mybir.ActivationFunctionType.Copy
+
+P = 128
+PACK = 4
+Q = 128
+K = 512
+COLS = 1024
+SLOTS = 512
+BANK = 512
+HALF = SLOTS // 2
+LIST_COLS = SLOTS // 16
+CAST_S = 48
+
+FLOPS = 2 * 512 * K * Q + 4 * 2 * 512 * Q * COLS
+
+
+def load_scales(queue, plane, scales):
+    for quad in range(4):
+        queue.dma_start(
+            out=plane[32 * quad : 32 * quad + 4, :].bitcast(I32),
+            in_=scales[0, 4 * quad : 4 * quad + 4, :].bitcast(I32),
+        )
+
+
+def tile_attend_ladderfour_madefour_kernel(
+    tc, states, wq_words, wq_scales, keys_words, keys_scales, notes_words, notes_scales,
+    users_words, users_scales, shelves_words, shelves_scales,
+    offs, offs2, offs3, offs4, offs5, offs6, out,
+):
+    nc = tc.nc
+    with ExitStack() as ctx:
+        sb = ctx.enter_context(tc.tile_pool(name="sb", bufs=1))
+        ps = ctx.enter_context(tc.psum_pool(name="ps", bufs=1))
+
+        def words8(name, src, n):
+            t = sb.tile([P, n], U32, name=name, align_bytes=64)
+            nc.sync.dma_start(out=t[:].bitcast(I32), in_=src[0].rearrange("p n t -> p (n t)").bitcast(I32))
+            return t
+
+        def words4(name, src, n):
+            t = sb.tile([P, 2 * n], U8, name=name, align_bytes=64)
+            nc.sync.dma_start(out=t[:].bitcast(I32), in_=src[0].bitcast(I32))
+            return t
+
+        def plane(name, src, n, queue):
+            t = sb.tile([P, n], U8, name=name, align_bytes=64)
+            load_scales(queue, t, src)
+            return t
+
+        def slot_list(name, src):
+            t = sb.tile([P, LIST_COLS], U16, name=name)
+            nc.sync.dma_start(t[:], src)
+            return t
+
+        def half(lst, h):
+            return lst[:, h * (LIST_COLS // 2) : (h + 1) * (LIST_COLS // 2)]
+
+        def cols(h):
+            return slice(h * HALF, (h + 1) * HALF)
+
+        wq_s = sb.tile([P, K], U8, name="wq_s", align_bytes=64)
+        nc.vector.memset(wq_s[:].bitcast(U32), 0)
+
+        raw = sb.tile([P, PACK, Q], F32, name="raw")
+        nc.sync.dma_start(out=raw[:], in_=states.rearrange("(p j) q -> p j q", j=PACK))
+        load_scales(nc.sync, wq_s, wq_scales)
+        wq_w = words8("wq_w", wq_words, K)
+        shelves_w = words4("shelves_w", shelves_words, COLS)
+        shelves_s = plane("shelves_s", shelves_scales, COLS, nc.sync)
+        keys_w = words8("keys_w", keys_words, COLS)
+        keys_s = plane("keys_s", keys_scales, COLS, nc.sync)
+        notes_w = words4("notes_w", notes_words, COLS)
+        notes_s = plane("notes_s", notes_scales, COLS, nc.gpsimd)
+        l_a = slot_list("l_a", offs)
+        l_b = slot_list("l_b", offs2)
+        l_f1 = slot_list("l_f1", offs3)
+        l_d = slot_list("l_d", offs5)
+        users_w = words8("users_w", users_words, COLS)
+        users_s = plane("users_s", users_scales, COLS, nc.sync)
+        l_c = slot_list("l_c", offs4)
+        l_f2 = slot_list("l_f2", offs6)
+
+        f1 = sb.tile([P, COLS], F32, name="f1")
+        f2 = sb.tile([P, COLS], F32, name="f2")
+        nc.vector.memset(f1[:], 0.0)
+        nc.vector.memset(f2[:], 0.0)
+
+        wq_sd = sb.tile([P, K], U8, name="wq_sd", align_bytes=64)
+        nc.vector.tensor_copy(
+            out=wq_sd[:].rearrange("p (t m) -> p m t", t=PACK), in_=wq_s[:].rearrange("p (m t) -> p m t", t=PACK)
+        )
+
+        st_bf = sb.tile([P, Q, PACK], BF16, name="st_bf", align_bytes=64)
+        by_q = raw[:].rearrange("p j q -> p q j")
+        nc.scalar.activation(out=st_bf[:, :CAST_S, :], in_=by_q[:, :CAST_S, :], func=COPY)
+        nc.vector.tensor_copy(out=st_bf[:, CAST_S:, :], in_=by_q[:, CAST_S:, :])
+        st_w = sb.tile([P, Q], U32, name="st_w", align_bytes=64)
+        st_s = sb.tile([P, Q], U8, name="st_s", align_bytes=64)
+        nc.vector.quantize_mx(out=st_w[:].bitcast(FP8X4), scales=st_s[:], in_=st_bf[:].rearrange("p q j -> p (q j)"))
+
+        wq_wd = [sb.tile([P, 2, P], U32, name="wq_wd" + str(u), align_bytes=64) for u in range(2)]
+        by_m = wq_w[:].rearrange("p (m t) -> p m t", t=PACK)
+        nc.vector.tensor_copy(out=wq_wd[0][:].rearrange("p t m -> p m t"), in_=by_m[:, :, 0:2])
+        nc.scalar.copy(out=wq_wd[1][:].rearrange("p t m -> p m t"), in_=by_m[:, :, 2:4])
+
+        def scores(name, tags, lw, ls, rw, rs, fp4):
+            banks = []
+            for h in range(COLS // BANK):
+                bank = ps.tile([P, BANK], F32, name=name + str(h), tag=tags[h])
+                c = slice(h * BANK, (h + 1) * BANK)
+                moving = rw[:, 2 * h * BANK : 2 * (h + 1) * BANK].bitcast(FP4X4) if fp4 else rw[:, c].bitcast(FP8X4)
+                nc.tensor.matmul_mx(
+                    out=bank[:], lhsT=lw[:].bitcast(FP8X4), lhsT_scale=ls[:],
+                    rhs=moving, rhs_scale=rs[:, c], start=True, stop=True,
+                )
+                banks.append(bank)
+            return banks
+
+        qv_ps = ps.tile([P, BANK], F32, name="qv_ps", tag="bank0")
+        for t in range(PACK):
+            c = slice(t * P, (t + 1) * P)
+            nc.tensor.matmul_mx(
+                out=qv_ps[:, c], lhsT=wq_wd[t // 2][:, t % 2, :].bitcast(FP8X4), lhsT_scale=wq_sd[:, c],
+                rhs=st_w[:].bitcast(FP8X4), rhs_scale=st_s[:], start=True, stop=True,
+            )
+        d_ps = scores("d_ps", ("bank5", "bank6"), st_w, st_s, shelves_w, shelves_s, True)
+        qv_bf = sb.tile([P, Q, PACK], BF16, name="qv_bf", align_bytes=64)
+        nc.scalar.activation(out=qv_bf[:], in_=qv_ps[:].rearrange("p (t q) -> p q t", t=PACK), func=COPY)
+        qv_w = sb.tile([P, Q], U32, name="qv_w", align_bytes=64)
+        qv_s = sb.tile([P, Q], U8, name="qv_s", align_bytes=64)
+        nc.vector.quantize_mx(out=qv_w[:].bitcast(FP8X4), scales=qv_s[:], in_=qv_bf[:].rearrange("p q j -> p (q j)"))
+
+        a_ps = scores("a_ps", ("bank1", "bank2"), qv_w, qv_s, keys_w, keys_s, False)
+        b_ps = scores("b_ps", ("bank3", "bank4"), qv_w, qv_s, notes_w, notes_s, True)
+        a = sb.tile([P, COLS], F32, name="a")
+        b = sb.tile([P, COLS], F32, name="b")
+        nc.vector.tensor_copy(out=a[:, :BANK], in_=a_ps[0][:])
+        nc.scalar.copy(out=a[:, BANK:], in_=a_ps[1][:])
+        nc.vector.tensor_copy(out=b[:, :BANK], in_=b_ps[0][:])
+        nc.scalar.copy(out=b[:, BANK:], in_=b_ps[1][:])
+
+        ga = sb.tile([P, SLOTS], F32, name="ga")
+        gb = [sb.tile([P, HALF], F32, name="gb" + str(h)) for h in range(2)]
+        nc.vector.tensor_copy(out=ga[:], in_=a[:].indirect(l_a[:]))
+        for h in range(2):
+            nc.scalar.activation(out=gb[h][:], in_=b[:].indirect(half(l_b, h)), func=COPY)
+        for h in range(2):
+            nc.vector.tensor_tensor(out=f1[:].indirect(half(l_f1, h)), in0=ga[:, cols(h)], in1=gb[h][:], op=ADD)
+
+        c_ps = scores("c_ps", ("bank7", "bank0"), st_w, st_s, users_w, users_s, False)
+        d0 = sb.tile([P, COLS], F32, name="d0")
+        for h in range(2):
+            nc.scalar.copy(out=d0[:, h * BANK : (h + 1) * BANK], in_=d_ps[h][:])
+        neg_d = sb.tile([P, SLOTS], F32, name="neg_d")
+        nc.scalar.activation(out=neg_d[:], in_=d0[:].indirect(l_d[:]), func=COPY, scale=-1.0)
+
+        cc = sb.tile([P, COLS], F32, name="cc")
+        for h in range(2):
+            c = slice(h * BANK, (h + 1) * BANK)
+            nc.vector.tensor_tensor(out=cc[:, c], in0=c_ps[h][:], in1=f1[:, c], op=ADD)
+        gc = sb.tile([P, SLOTS], F32, name="gc")
+        nc.vector.tensor_copy(out=gc[:, cols(0)], in_=cc[:].indirect(half(l_c, 0)))
+        nc.scalar.activation(out=gc[:, cols(1)], in_=cc[:].indirect(half(l_c, 1)), func=COPY)
+        nc.vector.tensor_tensor(out=f2[:].indirect(l_f2[:]), in0=gc[:], in1=neg_d[:], op=ADD)
+
+        dd = sb.tile([P, COLS], F32, name="dd")
+        nc.vector.tensor_tensor(out=dd[:], in0=d0[:], in1=f2[:], op=ADD)
+        y = [sb.tile([P, HALF], F32, name="y" + str(h)) for h in range(2)]
+        nc.vector.tensor_copy(out=y[0][:], in_=dd[:].indirect(half(l_d, 0)))
+        nc.scalar.activation(out=y[1][:], in_=dd[:].indirect(half(l_d, 1)), func=COPY)
+        nc.sync.dma_start(out=out[:, cols(0)], in_=y[0][:])
+        nc.scalar.dma_start(out=out[:, cols(1)], in_=y[1][:])

@@ -23,14 +23,15 @@ BANK = 512
 HALF = SLOTS // 2
 LIST_COLS = SLOTS // 16
 CAST_S = 48
+WQ_ROW, KEYS_ROW, USERS_ROW = 12, 4, 8
 
 FLOPS = 2 * 512 * K * Q + 4 * 2 * 512 * Q * COLS
 
 
-def load_scales(queue, plane, scales):
+def load_scales(nc, plane, first, scales):
     for quad in range(4):
-        queue.dma_start(
-            out=plane[32 * quad : 32 * quad + 4, :].bitcast(I32),
+        nc.sync.dma_start(
+            out=plane[32 * quad + first : 32 * quad + first + 4, :].bitcast(I32),
             in_=scales[0, 4 * quad : 4 * quad + 4, :].bitcast(I32),
         )
 
@@ -55,10 +56,10 @@ def tile_attend_ladderfour_madefour_kernel(
             nc.sync.dma_start(out=t[:].bitcast(I32), in_=src[0].bitcast(I32))
             return t
 
-        def plane(name, src, n, queue):
+        def plane(name, src, n, first):
             t = sb.tile([P, n], U8, name=name, align_bytes=64)
-            load_scales(queue, t, src)
-            return t
+            load_scales(nc, t, first, src)
+            return t[first:, :]
 
         def slot_list(name, src):
             t = sb.tile([P, LIST_COLS], U16, name=name)
@@ -76,20 +77,20 @@ def tile_attend_ladderfour_madefour_kernel(
 
         raw = sb.tile([P, PACK, Q], F32, name="raw")
         nc.sync.dma_start(out=raw[:], in_=states.rearrange("(p j) q -> p j q", j=PACK))
-        load_scales(nc.sync, wq_s, wq_scales)
+        load_scales(nc, wq_s, WQ_ROW, wq_scales)
         wq_w = words8("wq_w", wq_words, K)
-        shelves_w = words4("shelves_w", shelves_words, COLS)
-        shelves_s = plane("shelves_s", shelves_scales, COLS, nc.sync)
         keys_w = words8("keys_w", keys_words, COLS)
-        keys_s = plane("keys_s", keys_scales, COLS, nc.sync)
+        keys_s = plane("keys_s", keys_scales, COLS, KEYS_ROW)
         notes_w = words4("notes_w", notes_words, COLS)
-        notes_s = plane("notes_s", notes_scales, COLS, nc.gpsimd)
+        notes_s = plane("notes_s", notes_scales, COLS, 0)
         l_a = slot_list("l_a", offs)
         l_b = slot_list("l_b", offs2)
         l_f1 = slot_list("l_f1", offs3)
+        shelves_w = words4("shelves_w", shelves_words, COLS)
+        shelves_s = plane("shelves_s", shelves_scales, COLS, 0)
         l_d = slot_list("l_d", offs5)
         users_w = words8("users_w", users_words, COLS)
-        users_s = plane("users_s", users_scales, COLS, nc.sync)
+        users_s = plane("users_s", users_scales, COLS, USERS_ROW)
         l_c = slot_list("l_c", offs4)
         l_f2 = slot_list("l_f2", offs6)
 
@@ -117,11 +118,12 @@ def tile_attend_ladderfour_madefour_kernel(
         nc.scalar.copy(out=wq_wd[1][:].rearrange("p t m -> p m t"), in_=by_m[:, :, 2:4])
 
         def scores(name, tags, lw, ls, rw, rs, fp4):
+            width = COLS // len(tags)
             banks = []
-            for h in range(COLS // BANK):
-                bank = ps.tile([P, BANK], F32, name=name + str(h), tag=tags[h])
-                c = slice(h * BANK, (h + 1) * BANK)
-                moving = rw[:, 2 * h * BANK : 2 * (h + 1) * BANK].bitcast(FP4X4) if fp4 else rw[:, c].bitcast(FP8X4)
+            for h, tag in enumerate(tags):
+                bank = ps.tile([P, width], F32, name=name + str(h), tag=tag)
+                c = slice(h * width, (h + 1) * width)
+                moving = rw[:, 2 * h * width : 2 * (h + 1) * width].bitcast(FP4X4) if fp4 else rw[:, c].bitcast(FP8X4)
                 nc.tensor.matmul_mx(
                     out=bank[:], lhsT=lw[:].bitcast(FP8X4), lhsT_scale=ls[:],
                     rhs=moving, rhs_scale=rs[:, c], start=True, stop=True,
@@ -133,10 +135,9 @@ def tile_attend_ladderfour_madefour_kernel(
         for t in range(PACK):
             c = slice(t * P, (t + 1) * P)
             nc.tensor.matmul_mx(
-                out=qv_ps[:, c], lhsT=wq_wd[t // 2][:, t % 2, :].bitcast(FP8X4), lhsT_scale=wq_sd[:, c],
+                out=qv_ps[:, c], lhsT=wq_wd[t // 2][:, t % 2, :].bitcast(FP8X4), lhsT_scale=wq_sd[WQ_ROW:, c],
                 rhs=st_w[:].bitcast(FP8X4), rhs_scale=st_s[:], start=True, stop=True,
             )
-        d_ps = scores("d_ps", ("bank5", "bank6"), st_w, st_s, shelves_w, shelves_s, True)
         qv_bf = sb.tile([P, Q, PACK], BF16, name="qv_bf", align_bytes=64)
         nc.scalar.activation(out=qv_bf[:], in_=qv_ps[:].rearrange("p (t q) -> p q t", t=PACK), func=COPY)
         qv_w = sb.tile([P, Q], U32, name="qv_w", align_bytes=64)
@@ -144,24 +145,26 @@ def tile_attend_ladderfour_madefour_kernel(
         nc.vector.quantize_mx(out=qv_w[:].bitcast(FP8X4), scales=qv_s[:], in_=qv_bf[:].rearrange("p q j -> p (q j)"))
 
         a_ps = scores("a_ps", ("bank1", "bank2"), qv_w, qv_s, keys_w, keys_s, False)
-        b_ps = scores("b_ps", ("bank3", "bank4"), qv_w, qv_s, notes_w, notes_s, True)
+        b_ps = scores("b_ps", ("bank3", "bank4", "bank5", "bank6"), qv_w, qv_s, notes_w, notes_s, True)
         a = sb.tile([P, COLS], F32, name="a")
-        b = sb.tile([P, COLS], F32, name="b")
-        nc.vector.tensor_copy(out=a[:, :BANK], in_=a_ps[0][:])
-        nc.scalar.copy(out=a[:, BANK:], in_=a_ps[1][:])
-        nc.vector.tensor_copy(out=b[:, :BANK], in_=b_ps[0][:])
-        nc.scalar.copy(out=b[:, BANK:], in_=b_ps[1][:])
+        b = sb.tile([P, COLS], F32, name="b", tag="b_then_d0")
+        for h, bank in enumerate(a_ps):
+            nc.scalar.copy(out=a[:, h * BANK : (h + 1) * BANK], in_=bank[:])
+        for h, bank in enumerate(b_ps):
+            nc.vector.tensor_copy(out=b[:, h * HALF : (h + 1) * HALF], in_=bank[:])
 
-        ga = sb.tile([P, SLOTS], F32, name="ga")
+        ga = [sb.tile([P, HALF], F32, name="ga" + str(h)) for h in range(2)]
         gb = [sb.tile([P, HALF], F32, name="gb" + str(h)) for h in range(2)]
-        nc.vector.tensor_copy(out=ga[:], in_=a[:].indirect(l_a[:]))
         for h in range(2):
-            nc.scalar.activation(out=gb[h][:], in_=b[:].indirect(half(l_b, h)), func=COPY)
+            nc.scalar.activation(out=ga[h][:], in_=a[:].indirect(half(l_a, h)), func=COPY)
+        nc.vector.tensor_copy(out=gb[0][:], in_=b[:].indirect(half(l_b, 0)))
+        nc.scalar.activation(out=gb[1][:], in_=b[:].indirect(half(l_b, 1)), func=COPY)
         for h in range(2):
-            nc.vector.tensor_tensor(out=f1[:].indirect(half(l_f1, h)), in0=ga[:, cols(h)], in1=gb[h][:], op=ADD)
+            nc.vector.tensor_tensor(out=f1[:].indirect(half(l_f1, h)), in0=ga[h][:], in1=gb[h][:], op=ADD)
 
+        d_ps = scores("d_ps", ("bank1", "bank2"), st_w, st_s, shelves_w, shelves_s, True)
         c_ps = scores("c_ps", ("bank7", "bank0"), st_w, st_s, users_w, users_s, False)
-        d0 = sb.tile([P, COLS], F32, name="d0")
+        d0 = sb.tile([P, COLS], F32, name="d0", tag="b_then_d0")
         for h in range(2):
             nc.scalar.copy(out=d0[:, h * BANK : (h + 1) * BANK], in_=d_ps[h][:])
         neg_d = sb.tile([P, SLOTS], F32, name="neg_d")

@@ -23,14 +23,15 @@ BANK = 512
 HALF = SLOTS // 2
 LIST_COLS = SLOTS // 16
 CAST_S = 48
+SPLIT = 688
 WQ_ROW, KEYS_ROW, USERS_ROW = 12, 4, 8
 
 FLOPS = 2 * 512 * K * Q + 4 * 2 * 512 * Q * COLS
 
 
-def load_scales(nc, plane, first, scales):
+def load_scales(queue, plane, first, scales):
     for quad in range(4):
-        nc.sync.dma_start(
+        queue.dma_start(
             out=plane[32 * quad + first : 32 * quad + first + 4, :].bitcast(I32),
             in_=scales[0, 4 * quad : 4 * quad + 4, :].bitcast(I32),
         )
@@ -46,8 +47,8 @@ def tile_attend_ladderfour_madefour_kernel(
         sb = ctx.enter_context(tc.tile_pool(name="sb", bufs=1))
         ps = ctx.enter_context(tc.psum_pool(name="ps", bufs=1))
 
-        def words8(name, src, n):
-            t = sb.tile([P, n], U32, name=name, align_bytes=64)
+        def words8(name, src, n, tag):
+            t = sb.tile([P, n], U32, name=name, tag=tag, align_bytes=64)
             nc.sync.dma_start(out=t[:].bitcast(I32), in_=src[0].rearrange("p n t -> p (n t)").bitcast(I32))
             return t
 
@@ -56,9 +57,9 @@ def tile_attend_ladderfour_madefour_kernel(
             nc.sync.dma_start(out=t[:].bitcast(I32), in_=src[0].bitcast(I32))
             return t
 
-        def plane(name, src, n, first):
+        def plane(name, src, n, first, queue):
             t = sb.tile([P, n], U8, name=name, align_bytes=64)
-            load_scales(nc, t, first, src)
+            load_scales(queue, t, first, src)
             return t[first:, :]
 
         def slot_list(name, src):
@@ -77,27 +78,22 @@ def tile_attend_ladderfour_madefour_kernel(
 
         raw = sb.tile([P, PACK, Q], F32, name="raw")
         nc.sync.dma_start(out=raw[:], in_=states.rearrange("(p j) q -> p j q", j=PACK))
-        load_scales(nc, wq_s, WQ_ROW, wq_scales)
-        wq_w = words8("wq_w", wq_words, K)
-        keys_w = words8("keys_w", keys_words, COLS)
-        keys_s = plane("keys_s", keys_scales, COLS, KEYS_ROW)
+        load_scales(nc.sync, wq_s, WQ_ROW, wq_scales)
+        wq_w = words8("wq_w", wq_words, K, "wq_w_then_f2")
+        shelves_w = words4("shelves_w", shelves_words, COLS)
+        shelves_s = plane("shelves_s", shelves_scales, COLS, 0, nc.sync)
+        keys_w = words8("keys_w", keys_words, COLS, "keys_w")
+        keys_s = plane("keys_s", keys_scales, COLS, KEYS_ROW, nc.sync)
         notes_w = words4("notes_w", notes_words, COLS)
-        notes_s = plane("notes_s", notes_scales, COLS, 0)
+        notes_s = plane("notes_s", notes_scales, COLS, 0, nc.gpsimd)
         l_a = slot_list("l_a", offs)
         l_b = slot_list("l_b", offs2)
         l_f1 = slot_list("l_f1", offs3)
-        shelves_w = words4("shelves_w", shelves_words, COLS)
-        shelves_s = plane("shelves_s", shelves_scales, COLS, 0)
         l_d = slot_list("l_d", offs5)
-        users_w = words8("users_w", users_words, COLS)
-        users_s = plane("users_s", users_scales, COLS, USERS_ROW)
+        users_w = words8("users_w", users_words, COLS, "users_w")
+        users_s = plane("users_s", users_scales, COLS, USERS_ROW, nc.sync)
         l_c = slot_list("l_c", offs4)
         l_f2 = slot_list("l_f2", offs6)
-
-        f1 = sb.tile([P, COLS], F32, name="f1")
-        f2 = sb.tile([P, COLS], F32, name="f2")
-        nc.vector.memset(f1[:], 0.0)
-        nc.vector.memset(f2[:], 0.0)
 
         wq_sd = sb.tile([P, K], U8, name="wq_sd", align_bytes=64)
         nc.vector.tensor_copy(
@@ -108,14 +104,14 @@ def tile_attend_ladderfour_madefour_kernel(
         by_q = raw[:].rearrange("p j q -> p q j")
         nc.scalar.activation(out=st_bf[:, :CAST_S, :], in_=by_q[:, :CAST_S, :], func=COPY)
         nc.vector.tensor_copy(out=st_bf[:, CAST_S:, :], in_=by_q[:, CAST_S:, :])
-        st_w = sb.tile([P, Q], U32, name="st_w", align_bytes=64)
-        st_s = sb.tile([P, Q], U8, name="st_s", align_bytes=64)
-        nc.vector.quantize_mx(out=st_w[:].bitcast(FP8X4), scales=st_s[:], in_=st_bf[:].rearrange("p q j -> p (q j)"))
-
-        wq_wd = [sb.tile([P, 2, P], U32, name="wq_wd" + str(u), align_bytes=64) for u in range(2)]
+        wq_wd = [sb.tile([P, 2, P], U32, name="wq_wd" + str(u), tag="wq_wd" + str(u), align_bytes=64) for u in range(2)]
         by_m = wq_w[:].rearrange("p (m t) -> p m t", t=PACK)
         nc.vector.tensor_copy(out=wq_wd[0][:].rearrange("p t m -> p m t"), in_=by_m[:, :, 0:2])
         nc.scalar.copy(out=wq_wd[1][:].rearrange("p t m -> p m t"), in_=by_m[:, :, 2:4])
+
+        st_w = sb.tile([P, Q], U32, name="st_w", align_bytes=64)
+        st_s = sb.tile([P, Q], U8, name="st_s", align_bytes=64)
+        nc.vector.quantize_mx(out=st_w[:].bitcast(FP8X4), scales=st_s[:], in_=st_bf[:].rearrange("p q j -> p (q j)"))
 
         def scores(name, tags, lw, ls, rw, rs, fp4):
             width = COLS // len(tags)
@@ -131,6 +127,11 @@ def tile_attend_ladderfour_madefour_kernel(
                 banks.append(bank)
             return banks
 
+        def add_rows(total, banks, tail, placed):
+            nc.gpsimd.tensor_tensor(out=total[:, SPLIT:], in0=tail, in1=placed[:, SPLIT:], op=ADD)
+            nc.vector.tensor_tensor(out=total[:, :BANK], in0=banks[0][:], in1=placed[:, :BANK], op=ADD)
+            nc.vector.tensor_tensor(out=total[:, BANK:SPLIT], in0=banks[1][:, : SPLIT - BANK], in1=placed[:, BANK:SPLIT], op=ADD)
+
         qv_ps = ps.tile([P, BANK], F32, name="qv_ps", tag="bank0")
         for t in range(PACK):
             c = slice(t * P, (t + 1) * P)
@@ -138,6 +139,11 @@ def tile_attend_ladderfour_madefour_kernel(
                 out=qv_ps[:, c], lhsT=wq_wd[t // 2][:, t % 2, :].bitcast(FP8X4), lhsT_scale=wq_sd[WQ_ROW:, c],
                 rhs=st_w[:].bitcast(FP8X4), rhs_scale=st_s[:], start=True, stop=True,
             )
+        d_ps = scores("d_ps", ("bank6", "bank7"), st_w, st_s, shelves_w, shelves_s, True)
+        f1 = sb.tile([P, COLS], F32, name="f1", tag="wq_wd0", align_bytes=64)
+        f2 = sb.tile([P, COLS], F32, name="f2", tag="wq_w_then_f2", align_bytes=64)
+        nc.vector.memset(f1[:], 0.0)
+        nc.vector.memset(f2[:], 0.0)
         qv_bf = sb.tile([P, Q, PACK], BF16, name="qv_bf", align_bytes=64)
         nc.scalar.activation(out=qv_bf[:], in_=qv_ps[:].rearrange("p (t q) -> p q t", t=PACK), func=COPY)
         qv_w = sb.tile([P, Q], U32, name="qv_w", align_bytes=64)
@@ -145,7 +151,7 @@ def tile_attend_ladderfour_madefour_kernel(
         nc.vector.quantize_mx(out=qv_w[:].bitcast(FP8X4), scales=qv_s[:], in_=qv_bf[:].rearrange("p q j -> p (q j)"))
 
         a_ps = scores("a_ps", ("bank1", "bank2"), qv_w, qv_s, keys_w, keys_s, False)
-        b_ps = scores("b_ps", ("bank3", "bank4", "bank5", "bank6"), qv_w, qv_s, notes_w, notes_s, True)
+        b_ps = scores("b_ps", ("bank3", "bank4", "bank5", "bank0"), qv_w, qv_s, notes_w, notes_s, True)
         a = sb.tile([P, COLS], F32, name="a")
         b = sb.tile([P, COLS], F32, name="b", tag="b_then_d0")
         for h, bank in enumerate(a_ps):
@@ -162,25 +168,24 @@ def tile_attend_ladderfour_madefour_kernel(
         for h in range(2):
             nc.vector.tensor_tensor(out=f1[:].indirect(half(l_f1, h)), in0=ga[h][:], in1=gb[h][:], op=ADD)
 
-        d_ps = scores("d_ps", ("bank1", "bank2"), st_w, st_s, shelves_w, shelves_s, True)
-        c_ps = scores("c_ps", ("bank7", "bank0"), st_w, st_s, users_w, users_s, False)
+        c_ps = scores("c_ps", ("bank1", "bank2"), st_w, st_s, users_w, users_s, False)
         d0 = sb.tile([P, COLS], F32, name="d0", tag="b_then_d0")
         for h in range(2):
             nc.scalar.copy(out=d0[:, h * BANK : (h + 1) * BANK], in_=d_ps[h][:])
+        c_tail = sb.tile([P, COLS - SPLIT], F32, name="c_tail")
+        nc.scalar.copy(out=c_tail[:], in_=c_ps[1][:, SPLIT - BANK :])
         neg_d = sb.tile([P, SLOTS], F32, name="neg_d")
         nc.scalar.activation(out=neg_d[:], in_=d0[:].indirect(l_d[:]), func=COPY, scale=-1.0)
 
         cc = sb.tile([P, COLS], F32, name="cc")
-        for h in range(2):
-            c = slice(h * BANK, (h + 1) * BANK)
-            nc.vector.tensor_tensor(out=cc[:, c], in0=c_ps[h][:], in1=f1[:, c], op=ADD)
+        add_rows(cc, c_ps, c_tail[:], f1)
         gc = sb.tile([P, SLOTS], F32, name="gc")
         nc.vector.tensor_copy(out=gc[:, cols(0)], in_=cc[:].indirect(half(l_c, 0)))
         nc.scalar.activation(out=gc[:, cols(1)], in_=cc[:].indirect(half(l_c, 1)), func=COPY)
         nc.vector.tensor_tensor(out=f2[:].indirect(l_f2[:]), in0=gc[:], in1=neg_d[:], op=ADD)
 
         dd = sb.tile([P, COLS], F32, name="dd")
-        nc.vector.tensor_tensor(out=dd[:], in0=d0[:], in1=f2[:], op=ADD)
+        add_rows(dd, d_ps, d0[:, SPLIT:], f2)
         y = [sb.tile([P, HALF], F32, name="y" + str(h)) for h in range(2)]
         nc.vector.tensor_copy(out=y[0][:], in_=dd[:].indirect(half(l_d, 0)))
         nc.scalar.activation(out=y[1][:], in_=dd[:].indirect(half(l_d, 1)), func=COPY)

from contextlib import ExitStack

import concourse.mybir as mybir

F32 = mybir.dt.float32
BF16 = mybir.dt.bfloat16
I32 = mybir.dt.int32
U32 = mybir.dt.uint32
U16 = mybir.dt.uint16
U8 = mybir.dt.uint8
FP8X4 = mybir.dt.float8_e4m3fn_x4
FP4X4 = mybir.dt.float4_e2m1fn_x4
ADD = mybir.AluOpType.add
COPY = mybir.ActivationFunctionType.Copy

P = 128
PACK = 4
Q = 128
K = 512
COLS = 1024
SLOTS = 512
BANK = 512
HALF = SLOTS // 2
LIST_COLS = SLOTS // 16
CAST_S = 48
SPLIT = 688
WQ_ROW, KEYS_ROW, USERS_ROW = 12, 4, 8

FLOPS = 2 * 512 * K * Q + 4 * 2 * 512 * Q * COLS


def load_scales(queue, plane, first, scales):
    for quad in range(4):
        queue.dma_start(
            out=plane[32 * quad + first : 32 * quad + first + 4, :].bitcast(I32),
            in_=scales[0, 4 * quad : 4 * quad + 4, :].bitcast(I32),
        )


def tile_attend_ladderfour_madefour_kernel(
    tc, states, wq_words, wq_scales, keys_words, keys_scales, notes_words, notes_scales,
    users_words, users_scales, shelves_words, shelves_scales,
    offs, offs2, offs3, offs4, offs5, offs6, out,
):
    nc = tc.nc
    with ExitStack() as ctx:
        sb = ctx.enter_context(tc.tile_pool(name="sb", bufs=1))
        ps = ctx.enter_context(tc.psum_pool(name="ps", bufs=1))

        def words8(name, src, n, tag):
            t = sb.tile([P, n], U32, name=name, tag=tag, align_bytes=64)
            nc.sync.dma_start(out=t[:].bitcast(I32), in_=src[0].rearrange("p n t -> p (n t)").bitcast(I32))
            return t

        def words4(name, src, n):
            t = sb.tile([P, 2 * n], U8, name=name, align_bytes=64)
            nc.sync.dma_start(out=t[:].bitcast(I32), in_=src[0].bitcast(I32))
            return t

        def plane(name, src, n, first, queue):
            t = sb.tile([P, n], U8, name=name, align_bytes=64)
            load_scales(queue, t, first, src)
            return t[first:, :]

        def slot_list(name, src):
            t = sb.tile([P, LIST_COLS], U16, name=name)
            nc.sync.dma_start(t[:], src)
            return t

        def half(lst, h):
            return lst[:, h * (LIST_COLS // 2) : (h + 1) * (LIST_COLS // 2)]

        def cols(h):
            return slice(h * HALF, (h + 1) * HALF)

        wq_s = sb.tile([P, K], U8, name="wq_s", align_bytes=64)
        nc.vector.memset(wq_s[:].bitcast(U32), 0)

        raw = sb.tile([P, PACK, Q], F32, name="raw")
        nc.sync.dma_start(out=raw[:], in_=states.rearrange("(p j) q -> p j q", j=PACK))
        load_scales(nc.sync, wq_s, WQ_ROW, wq_scales)
        wq_w = words8("wq_w", wq_words, K, "wq_w_then_f2")
        shelves_w = words4("shelves_w", shelves_words, COLS)
        shelves_s = plane("shelves_s", shelves_scales, COLS, 0, nc.sync)
        keys_w = words8("keys_w", keys_words, COLS, "keys_w")
        keys_s = plane("keys_s", keys_scales, COLS, KEYS_ROW, nc.sync)
        notes_w = words4("notes_w", notes_words, COLS)
        notes_s = plane("notes_s", notes_scales, COLS, 0, nc.gpsimd)
        l_a = slot_list("l_a", offs)
        l_b = slot_list("l_b", offs2)
        l_f1 = slot_list("l_f1", offs3)
        l_d = slot_list("l_d", offs5)
        users_w = words8("users_w", users_words, COLS, "users_w")
        users_s = plane("users_s", users_scales, COLS, USERS_ROW, nc.sync)
        l_c = slot_list("l_c", offs4)
        l_f2 = slot_list("l_f2", offs6)

        wq_sd = sb.tile([P, K], U8, name="wq_sd", align_bytes=64)
        nc.vector.tensor_copy(
            out=wq_sd[:].rearrange("p (t m) -> p m t", t=PACK), in_=wq_s[:].rearrange("p (m t) -> p m t", t=PACK)
        )

        st_bf = sb.tile([P, Q, PACK], BF16, name="st_bf", align_bytes=64)
        by_q = raw[:].rearrange("p j q -> p q j")
        nc.scalar.activation(out=st_bf[:, :CAST_S, :], in_=by_q[:, :CAST_S, :], func=COPY)
        nc.vector.tensor_copy(out=st_bf[:, CAST_S:, :], in_=by_q[:, CAST_S:, :])
        wq_wd = [sb.tile([P, 2, P], U32, name="wq_wd" + str(u), tag="wq_wd" + str(u), align_bytes=64) for u in range(2)]
        by_m = wq_w[:].rearrange("p (m t) -> p m t", t=PACK)
        nc.vector.tensor_copy(out=wq_wd[0][:].rearrange("p t m -> p m t"), in_=by_m[:, :, 0:2])
        nc.scalar.copy(out=wq_wd[1][:].rearrange("p t m -> p m t"), in_=by_m[:, :, 2:4])

        st_w = sb.tile([P, Q], U32, name="st_w", align_bytes=64)
        st_s = sb.tile([P, Q], U8, name="st_s", align_bytes=64)
        nc.vector.quantize_mx(out=st_w[:].bitcast(FP8X4), scales=st_s[:], in_=st_bf[:].rearrange("p q j -> p (q j)"))

        def scores(name, tags, lw, ls, rw, rs, fp4):
            width = COLS // len(tags)
            banks = []
            for h, tag in enumerate(tags):
                bank = ps.tile([P, width], F32, name=name + str(h), tag=tag)
                c = slice(h * width, (h + 1) * width)
                moving = rw[:, 2 * h * width : 2 * (h + 1) * width].bitcast(FP4X4) if fp4 else rw[:, c].bitcast(FP8X4)
                nc.tensor.matmul_mx(
                    out=bank[:], lhsT=lw[:].bitcast(FP8X4), lhsT_scale=ls[:],
                    rhs=moving, rhs_scale=rs[:, c], start=True, stop=True,
                )
                banks.append(bank)
            return banks

        def add_rows(total, banks, tail, placed):
            nc.gpsimd.tensor_tensor(out=total[:, SPLIT:], in0=tail, in1=placed[:, SPLIT:], op=ADD)
            nc.vector.tensor_tensor(out=total[:, :BANK], in0=banks[0][:], in1=placed[:, :BANK], op=ADD)
            nc.vector.tensor_tensor(out=total[:, BANK:SPLIT], in0=banks[1][:, : SPLIT - BANK], in1=placed[:, BANK:SPLIT], op=ADD)

        qv_ps = ps.tile([P, BANK], F32, name="qv_ps", tag="bank0")
        for t in range(PACK):
            c = slice(t * P, (t + 1) * P)
            nc.tensor.matmul_mx(
                out=qv_ps[:, c], lhsT=wq_wd[t // 2][:, t % 2, :].bitcast(FP8X4), lhsT_scale=wq_sd[WQ_ROW:, c],
                rhs=st_w[:].bitcast(FP8X4), rhs_scale=st_s[:], start=True, stop=True,
            )
        d_ps = scores("d_ps", ("bank6", "bank7"), st_w, st_s, shelves_w, shelves_s, True)
        f1 = sb.tile([P, COLS], F32, name="f1", tag="wq_wd0", align_bytes=64)
        f2 = sb.tile([P, COLS], F32, name="f2", tag="wq_w_then_f2", align_bytes=64)
        nc.vector.memset(f1[:], 0.0)
        nc.vector.memset(f2[:], 0.0)
        qv_bf = sb.tile([P, Q, PACK], BF16, name="qv_bf", align_bytes=64)
        nc.scalar.activation(out=qv_bf[:], in_=qv_ps[:].rearrange("p (t q) -> p q t", t=PACK), func=COPY)
        qv_w = sb.tile([P, Q], U32, name="qv_w", align_bytes=64)
        qv_s = sb.tile([P, Q], U8, name="qv_s", align_bytes=64)
        nc.vector.quantize_mx(out=qv_w[:].bitcast(FP8X4), scales=qv_s[:], in_=qv_bf[:].rearrange("p q j -> p (q j)"))

        a_ps = scores("a_ps", ("bank1", "bank2"), qv_w, qv_s, keys_w, keys_s, False)
        b_ps = scores("b_ps", ("bank3", "bank4", "bank5", "bank0"), qv_w, qv_s, notes_w, notes_s, True)
        a = sb.tile([P, COLS], F32, name="a")
        b = sb.tile([P, COLS], F32, name="b", tag="b_then_d0")
        for h, bank in enumerate(a_ps):
            nc.scalar.copy(out=a[:, h * BANK : (h + 1) * BANK], in_=bank[:])
        for h, bank in enumerate(b_ps):
            nc.vector.tensor_copy(out=b[:, h * HALF : (h + 1) * HALF], in_=bank[:])

        ga = [sb.tile([P, HALF], F32, name="ga" + str(h)) for h in range(2)]
        gb = [sb.tile([P, HALF], F32, name="gb" + str(h)) for h in range(2)]
        for h in range(2):
            nc.scalar.activation(out=ga[h][:], in_=a[:].indirect(half(l_a, h)), func=COPY)
        nc.vector.tensor_copy(out=gb[0][:], in_=b[:].indirect(half(l_b, 0)))
        nc.scalar.activation(out=gb[1][:], in_=b[:].indirect(half(l_b, 1)), func=COPY)
        for h in range(2):
            nc.vector.tensor_tensor(out=f1[:].indirect(half(l_f1, h)), in0=ga[h][:], in1=gb[h][:], op=ADD)

        c_ps = scores("c_ps", ("bank1", "bank2"), st_w, st_s, users_w, users_s, False)
        d0 = sb.tile([P, COLS], F32, name="d0", tag="b_then_d0")
        for h in range(2):
            nc.scalar.copy(out=d0[:, h * BANK : (h + 1) * BANK], in_=d_ps[h][:])
        c_tail = sb.tile([P, COLS - SPLIT], F32, name="c_tail")
        nc.scalar.copy(out=c_tail[:], in_=c_ps[1][:, SPLIT - BANK :])
        neg_d = sb.tile([P, SLOTS], F32, name="neg_d")
        nc.scalar.activation(out=neg_d[:], in_=d0[:].indirect(l_d[:]), func=COPY, scale=-1.0)

        cc = sb.tile([P, COLS], F32, name="cc")
        add_rows(cc, c_ps, c_tail[:], f1)
        gc = sb.tile([P, SLOTS], F32, name="gc")
        nc.vector.tensor_copy(out=gc[:, cols(0)], in_=cc[:].indirect(half(l_c, 0)))
        nc.scalar.activation(out=gc[:, cols(1)], in_=cc[:].indirect(half(l_c, 1)), func=COPY)
        nc.vector.tensor_tensor(out=f2[:].indirect(l_f2[:]), in0=gc[:], in1=neg_d[:], op=ADD)

        dd = sb.tile([P, COLS], F32, name="dd")
        add_rows(dd, d_ps, d0[:, SPLIT:], f2)
        y = [sb.tile([P, HALF], F32, name="y" + str(h)) for h in range(2)]
        nc.vector.tensor_copy(out=y[0][:], in_=dd[:].indirect(half(l_d, 0)))
        nc.scalar.activation(out=y[1][:], in_=dd[:].indirect(half(l_d, 1)), func=COPY)
        nc.sync.dma_start(out=out[:, cols(0)], in_=y[0][:])
        nc.scalar.dma_start(out=out[:, cols(1)], in_=y[1][:])
